import numpy as np
import ml_dtypes


def mxq(x, axis, fmt="e4m3"):
    dtype, down = {"e4m3": (ml_dtypes.float8_e4m3fn, 7), "e5m2": (ml_dtypes.float8_e5m2, 14)}[fmt]
    v = np.moveaxis(np.asarray(x, np.float32).astype(ml_dtypes.bfloat16).astype(np.float64), axis, -1)
    blocks = v.reshape(v.shape[:-1] + (-1, 32))
    amax = np.abs(blocks).max(-1, keepdims=True)
    byte = np.maximum(np.where(amax > 0, np.frexp(amax)[1] - 1 + 127, 0) - down, 1)
    scale = np.exp2(byte - 127.0)
    codes = (blocks / scale).astype(np.float32).astype(dtype).astype(np.float64)
    return np.moveaxis((codes * scale).reshape(v.shape), -1, axis)


WIDE = False


def mx_kscale(k):
    if not WIDE:
        return np.ones(k)
    levels = np.array([10, -10, 5, -5, 0])
    if k % 512:
        return np.exp2(np.random.permutation(np.resize(levels, k // 32))).repeat(32)
    a = np.empty((k // 512, 16))
    for p in range(k // 512):
        a[p, :8] = np.random.permutation(np.resize(levels, 8))
        for g in range(8):
            far = levels[np.abs(levels - a[p, g]) >= 10]
            a[p, g + 8] = far[np.random.randint(len(far))]
    return np.exp2(a.ravel()).repeat(32)


def f64(x):
    return np.asarray(x).astype(np.float64)


def striped(idx):
    return np.tile(idx.reshape(-1, 16).T, (8, 1)).astype(np.uint16)


def unstriped(offs):
    return offs[:16].T.reshape(-1).astype(np.int64)


def striped8(idx):
    return np.concatenate([x.reshape(-1, 16).T for x in idx]).astype(np.uint16)


def runs(offs, k):
    lists = np.stack([offs[16 * r : 16 * r + 16].T.reshape(-1) for r in range(8)]).astype(np.int64)
    return lists[np.arange(k) % 512 // 64]


def pack_weight(w):
    k, n = w.shape
    w = f64(np.asarray(w, np.float32).astype(ml_dtypes.bfloat16)).reshape(k // 32, 32, n)
    amax = np.abs(w).max(1)
    byte = np.clip(np.where(amax > 0, np.frexp(amax)[1] - 1 + 127 - 7, 1), 1, 254)
    scaled = (w * np.exp2(127.0 - byte)[:, None, :]).reshape(k, n).astype(np.float32)
    words = np.ascontiguousarray(scaled.reshape(k // 512, 128, 4, n).transpose(0, 1, 3, 2)).astype(ml_dtypes.float8_e4m3fn).view(np.uint8)
    return words, np.ascontiguousarray(byte.astype(np.uint8).reshape(k // 512, 16, n))


def unpack_weight(words, scales):
    g, p, n, _ = words.shape
    vals = np.ascontiguousarray(words).view(ml_dtypes.float8_e4m3fn).astype(np.float64) * np.repeat(np.exp2(scales.astype(np.float64) - 127.0), 8, axis=1)[..., None]
    return vals.transpose(0, 1, 3, 2).reshape(g * 512, n)


K, T, S, G, H, W, C = 512, 1024, 256, 2048, 512, 128, 512


def setup_inputs():
    n = np.random.standard_normal
    s = mx_kscale(K)[:, None]
    packed_xT = pack_weight(n((K, T)) * s)
    packed_dT = pack_weight(n((K, G)) / s)
    perm = np.random.permutation(S)
    return {
        "x_words": packed_xT[0],
        "x_scales": packed_xT[1],
        "d_words": packed_dT[0],
        "d_scales": packed_dT[1],
        "gs": (np.random.uniform(0.5, 1.5, (K, 1)) / s).astype(np.float32),
        "offs": striped8(np.random.randint(0, T, (8, S))),
        "k1": striped8(np.random.randint(0, G, (8, H))),
        "n1": striped(perm[:W]),
        "n2": striped(perm[W:]),
        "n3": striped(np.random.permutation(S)),
        "cand": striped8(np.random.randint(0, T, (8, C))),
        "n4": striped(np.random.permutation(S)),
        "n5": striped(np.random.permutation(S)),
    }


def reference(x_words, x_scales, d_words, d_scales, gs, offs, k1, n1, n2, n3, cand, n4, n5):
    x_cand = unpack_weight(x_words, x_scales)[np.arange(K)[:, None], runs(cand, K)]
    d_k1 = unpack_weight(d_words, d_scales)[np.arange(K)[:, None], runs(k1, K)]
    xq = unpack_weight(x_words, x_scales)[np.arange(K)[:, None], runs(offs, K)]
    h = 0.0625 * (d_k1.T @ xq)
    pa = h[:, unstriped(n1)]
    pb = h[:, unstriped(n2)]
    rb = pa - pb
    ra = pa + pb
    ds = np.zeros((H, S))
    ds[:, unstriped(n1)] = ra
    dt = ds.copy()
    dt[:, unstriped(n2)] = rb
    z = f64(gs) * (np.maximum(dt, dt[:, unstriped(n3)]))
    s = 0.0625 * ((x_cand.T @ mxq(z, 0, "e4m3")))
    ds2 = np.zeros((C, S))
    ds2[:, unstriped(n4)] = s
    ds3 = np.zeros((C, S))
    ds3[:, unstriped(n5)] = s
    return np.maximum(ds2, ds3)

@@ -1,0 +1,225 @@
+from contextlib import ExitStack
+
+import concourse.mybir as mybir
+
+K, T, S, G, H, W, C = 512, 1024, 256, 2048, 512, 128, 512
+FLOPS = 2 * K * H * S + 2 * K * C * S
+
+F32 = mybir.dt.float32
+BF16 = mybir.dt.bfloat16
+I32 = mybir.dt.int32
+U32 = mybir.dt.uint32
+U16 = mybir.dt.uint16
+U8 = mybir.dt.uint8
+FP8X4 = mybir.dt.float8_e4m3fn_x4
+ALU = mybir.AluOpType
+COPY = mybir.ActivationFunctionType.Copy
+
+P = 128
+PACK = 4
+HALF = S // 2
+SPLIT_BLOCKS = 2
+
+
+def tile_picked_hpqhhaarhsendtwo_none_p_kernel(
+    tc, x_words, x_scales, d_words, d_scales, gs, offs, k1, n1, n2, n3, cand, n4, n5, out
+):
+    nc = tc.nc
+    with ExitStack() as ctx:
+        keep = ctx.enter_context(tc.tile_pool(name="keep", bufs=1))
+        psum = ctx.enter_context(tc.psum_pool(name="psum", bufs=1))
+
+        def load_list(name, dram):
+            held = keep.tile(list(dram.shape), U16, name=name)
+            nc.sync.dma_start(held[:], dram)
+            return held
+
+        def load_words(name, dram, width):
+            held = keep.tile([P, width], U32, name=name, align_bytes=64)
+            nc.sync.dma_start(held[:].bitcast(I32), dram[0].rearrange("p n t -> p (n t)").bitcast(I32))
+            return held
+
+        def load_scales(name, dram, width):
+            held = keep.tile([P, width], U8, name=name, align_bytes=64)
+            nc.vector.memset(held[:].bitcast(I32), 0)
+            nc.scalar.dma_start(held[0:P:8, :].bitcast(I32), dram[0].bitcast(I32))
+            return held
+
+        def zeroed_plane(name, width):
+            plane = keep.tile([P, width], U8, name=name, align_bytes=64)
+            nc.vector.memset(plane[:].bitcast(I32), 0)
+            return plane
+
+        def place_scale_rows(plane, picked, queue):
+            for i in range(4):
+                queue.dma_start(plane[i:P:32, :].bitcast(I32), picked[8 * i:P:32, :].bitcast(I32))
+
+        xs_table = load_scales("xs_table", x_scales, T)
+        ds_table = load_scales("ds_table", d_scales, G)
+        k1_list = load_list("k1_list", k1)
+        offs_list = load_list("offs_list", offs)
+        n1_list = load_list("n1_list", n1)
+        n2_list = load_list("n2_list", n2)
+        n3_list = load_list("n3_list", n3)
+        dw_table = load_words("dw_table", d_words, G)
+        cand_list = load_list("cand_list", cand)
+        xw_table = load_words("xw_table", x_words, T)
+        n4_list = load_list("n4_list", n4)
+        n5_list = load_list("n5_list", n5)
+        gs_raw = keep.tile([P, PACK], F32, name="gs_raw")
+        nc.gpsimd.dma_start(gs_raw[:], gs.rearrange("(p t) o -> p (t o)", t=PACK))
+        first_plane = zeroed_plane("first_plane", H + S)
+        cand_plane = zeroed_plane("cand_plane", C)
+
+        gain = keep.tile([P, PACK], F32, name="gain")
+        nc.scalar.activation(out=gain[:], in_=gs_raw[:], func=COPY, scale=0.0625)
+
+        first_picked = keep.tile([P, H + S], U8, name="first_picked", align_bytes=64)
+        nc.vector.tensor_copy(out=first_picked[:, H:], in_=xs_table[:].indirect(offs_list[:]))
+        nc.vector.tensor_copy(out=first_picked[:, :H], in_=ds_table[:].indirect(k1_list[:]))
+        place_scale_rows(first_plane, first_picked, nc.scalar)
+
+        dw_picked = keep.tile([P, H], U32, name="dw_picked", tag="ds_table", align_bytes=64)
+        nc.vector.tensor_copy(out=dw_picked[:], in_=dw_table[:].indirect(k1_list[:]))
+        xq_words = keep.tile([P, S], U32, name="xq_words", align_bytes=64)
+        nc.vector.tensor_copy(out=xq_words[:], in_=xw_table[:].indirect(offs_list[:]))
+
+        dw_dealt = keep.tile([P, PACK, P], U32, name="dw_dealt", align_bytes=64)
+        ds_dealt = keep.tile([P, PACK, P], U8, name="ds_dealt", align_bytes=64)
+        dw_by_slot = dw_picked[:].rearrange("p (m t) -> p t m", t=PACK)
+        ds_by_slot = first_plane[:, :H].rearrange("p (m t) -> p t m", t=PACK)
+        for slots in (slice(0, 1), slice(1, PACK)):
+            nc.vector.tensor_copy(out=dw_dealt[:, slots, :], in_=dw_by_slot[:, slots, :])
+            nc.vector.tensor_copy(out=ds_dealt[:, slots, :], in_=ds_by_slot[:, slots, :])
+
+        h_rows = []
+        for t in range(PACK):
+            bank = psum.tile([P, S], F32, name=f"h_bank{t}", tag=f"bank{t}")
+            nc.tensor.matmul_mx(
+                out=bank[:],
+                lhsT=dw_dealt[:, t, :].bitcast(FP8X4),
+                lhsT_scale=ds_dealt[:, t, :],
+                rhs=xq_words[:].bitcast(FP8X4),
+                rhs_scale=first_plane[:, H:],
+                start=True,
+                stop=True,
+            )
+            h = keep.tile([P, S], F32, name=f"h{t}")
+            if t == 0:
+                nc.scalar.activation(out=h[:], in_=bank[:], func=COPY)
+            else:
+                nc.vector.tensor_copy(out=h[:], in_=bank[:])
+            h_rows.append(h)
+
+        mixed = [None] * PACK
+        dt_rows = [keep.tile([P, S], F32, name=f"dt{t}") for t in range(PACK)]
+        z_halves = [keep.tile([P, HALF, PACK], BF16, name=f"z_half{u}", align_bytes=64) for u in range(2)]
+
+        def fetch_pairs(t):
+            pair = keep.tile([P, 2, W], F32, name=f"pair{t}", align_bytes=64)
+            nc.scalar.activation(out=pair[:, 0, :], in_=h_rows[t][:].indirect(n1_list[:]), func=COPY)
+            nc.scalar.activation(out=pair[:, 1, :], in_=h_rows[t][:].indirect(n2_list[:]), func=COPY)
+            mix = keep.tile([P, 2, W], F32, name=f"mix{t}")
+            nc.vector.tensor_tensor(out=mix[:, 0, :], in0=pair[:, 0, :], in1=pair[:, 1, :], op=ALU.add)
+            nc.vector.tensor_tensor(out=mix[:, 1, :], in0=pair[:, 0, :], in1=pair[:, 1, :], op=ALU.subtract)
+            mixed[t] = mix
+
+        def send_pairs(ts):
+            for side, places in enumerate((n1_list, n2_list)):
+                for t in ts:
+                    nc.scalar.activation(out=dt_rows[t][:].indirect(places[:]), in_=mixed[t][:, side, :], func=COPY)
+
+        def make_z(t, u, other):
+            nc.scalar.activation(
+                out=other, in_=dt_rows[t][:].indirect(n3_list[:, 8 * u:8 * (u + 1)]), func=COPY
+            )
+            larger = keep.tile([P, HALF], F32, name=f"larger{t}_{u}")
+            nc.vector.tensor_tensor(out=larger[:], in0=other, in1=dt_rows[t][:, HALF * u:HALF * (u + 1)], op=ALU.max)
+            nc.vector.tensor_scalar(
+                out=z_halves[u][:, :, t], in0=larger[:], scalar1=gain[:, t:t + 1], scalar2=None, op0=ALU.mult
+            )
+
+        z_words = keep.tile([P, S], U32, name="z_words", align_bytes=64)
+        z_plane = zeroed_plane("z_plane", S)
+
+        def quantise_half(u):
+            cols = slice(HALF * u, HALF * (u + 1))
+            nc.vector.quantize_mx(
+                out=z_words[:, cols].bitcast(FP8X4),
+                scales=z_plane[:, cols],
+                in_=z_halves[u][:].rearrange("p j t -> p (j t)"),
+            )
+
+        early_other = keep.tile([P, PACK, HALF], F32, name="early_other")
+        fetch_pairs(0)
+        fetch_pairs(1)
+        cand_picked = keep.tile([P, C], U8, name="cand_picked", tag="pair0", align_bytes=64)
+        nc.vector.tensor_copy(out=cand_picked[:], in_=xs_table[:].indirect(cand_list[:]))
+        place_scale_rows(cand_plane, cand_picked, nc.sync)
+        send_pairs((0, 1))
+        fetch_pairs(2)
+        fetch_pairs(3)
+        cand_words = keep.tile([P, C], U32, name="cand_words", tag="pair2", align_bytes=64)
+        nc.vector.tensor_copy(out=cand_words[:], in_=xw_table[:].indirect(cand_list[:]))
+        make_z(0, 0, early_other[:, 0, :])
+        make_z(1, 0, early_other[:, 1, :])
+        send_pairs((2, 3))
+        make_z(2, 0, early_other[:, 2, :])
+        make_z(3, 0, early_other[:, 3, :])
+        quantise_half(0)
+
+        scores = [keep.tile([P, S], F32, name=f"scores{c}") for c in range(C // P)]
+
+        def score(c, cols, bank_tag):
+            width = cols.stop - cols.start
+            bank = psum.tile([P, width], F32, name=f"s_bank{c}_{cols.start}", tag=bank_tag)
+            nc.tensor.matmul_mx(
+                out=bank[:],
+                lhsT=cand_words[:, P * c:P * (c + 1)].bitcast(FP8X4),
+                lhsT_scale=cand_plane[:, P * c:P * (c + 1)],
+                rhs=z_words[:, cols].bitcast(FP8X4),
+                rhs_scale=z_plane[:, cols],
+                start=True,
+                stop=True,
+            )
+            nc.vector.tensor_scalar(out=scores[c][:, cols], in0=bank[:], scalar1=0.0625, scalar2=None, op0=ALU.mult)
+
+        sent = {}
+        for c in range(C // P):
+            width = S if c < SPLIT_BLOCKS else 2 * S
+            for side in range(2):
+                sent[c, side] = keep.tile([P, width], F32, name=f"sent{c}_{side}")
+
+        def send_scores(c, cols):
+            for side, places in enumerate((n4_list, n5_list)):
+                nc.scalar.activation(
+                    out=sent[c, side][:].indirect(places[:, cols.start // 16:cols.stop // 16]),
+                    in_=scores[c][:, cols],
+                    func=COPY,
+                )
+
+        def finish(c):
+            result = keep.tile([P, S], F32, name=f"result{c}")
+            nc.vector.tensor_tensor(out=result[:], in0=sent[c, 0][:, :S], in1=sent[c, 1][:, :S], op=ALU.max)
+            nc.sync.dma_start(out[P * c:P * (c + 1), :], result[:])
+
+        for c in range(SPLIT_BLOCKS):
+            score(c, slice(0, HALF), f"bank{c}")
+
+        late_other = keep.tile([P, PACK, HALF], F32, name="late_other", tag="mix3")
+        for t in range(PACK):
+            make_z(t, 1, late_other[:, t, :])
+        quantise_half(1)
+
+        for c in range(SPLIT_BLOCKS):
+            send_scores(c, slice(0, HALF))
+        for c in range(SPLIT_BLOCKS):
+            score(c, slice(HALF, S), f"bank{SPLIT_BLOCKS + c}")
+        for c in range(SPLIT_BLOCKS, C // P):
+            score(c, slice(0, S), f"bank{SPLIT_BLOCKS + c}")
+        for c in range(SPLIT_BLOCKS):
+            send_scores(c, slice(HALF, S))
+            finish(c)
+        for c in range(SPLIT_BLOCKS, C // P):
+            send_scores(c, slice(0, S))
+            finish(c)

@@ -17,8 +17,9 @@ COPY = mybir.ActivationFunctionType.Copy
 
 P = 128
 PACK = 4
-HALF = S // 2
-SPLIT_BLOCKS = 2
+EARLY = 64
+LATE = S - EARLY
+DW_FIRST = G // 4
 
 
 def tile_picked_hpqhhaarhsendtwo_none_p_kernel(
@@ -34,14 +35,14 @@ def tile_picked_hpqhhaarhsendtwo_none_p_kernel(
             nc.sync.dma_start(held[:], dram)
             return held
 
-        def load_words(name, dram, width):
-            held = keep.tile([P, width], U32, name=name, align_bytes=64)
-            nc.sync.dma_start(held[:].bitcast(I32), dram[0].rearrange("p n t -> p (n t)").bitcast(I32))
-            return held
+        def load_words(queue, held, dram, cols):
+            queue.dma_start(held[:, cols].bitcast(I32), dram[0].rearrange("p n t -> p (n t)").bitcast(I32)[:, cols])
 
-        def load_scales(name, dram, width):
+        def load_scales(name, dram, width, zeroers):
             held = keep.tile([P, width], U8, name=name, align_bytes=64)
-            nc.vector.memset(held[:].bitcast(I32), 0)
+            share = width // len(zeroers)
+            for n, engine in enumerate(zeroers):
+                engine.memset(held[:, n * share:(n + 1) * share].bitcast(I32), 0)
             nc.scalar.dma_start(held[0:P:8, :].bitcast(I32), dram[0].bitcast(I32))
             return held
 
@@ -50,34 +51,34 @@ def tile_picked_hpqhhaarhsendtwo_none_p_kernel(
             nc.vector.memset(plane[:].bitcast(I32), 0)
             return plane
 
-        def place_scale_rows(plane, picked, queue):
+        def place_scale_rows(plane, picked, queues):
             for i in range(4):
-                queue.dma_start(plane[i:P:32, :].bitcast(I32), picked[8 * i:P:32, :].bitcast(I32))
+                queues[i % len(queues)].dma_start(plane[i:P:32, :].bitcast(I32), picked[8 * i:P:32, :].bitcast(I32))
 
-        xs_table = load_scales("xs_table", x_scales, T)
-        ds_table = load_scales("ds_table", d_scales, G)
+        ds_table = load_scales("ds_table", d_scales, G, (nc.vector, nc.gpsimd))
+        xs_table = load_scales("xs_table", x_scales, T, (nc.vector,))
+        dw_table = keep.tile([P, G], U32, name="dw_table", align_bytes=64)
+        xw_table = keep.tile([P, T], U32, name="xw_table", align_bytes=64)
+        load_words(nc.scalar, dw_table, d_words, slice(0, DW_FIRST))
+        load_words(nc.scalar, dw_table, d_words, slice(DW_FIRST, G))
+        load_words(nc.scalar, xw_table, x_words, slice(0, T))
         k1_list = load_list("k1_list", k1)
         offs_list = load_list("offs_list", offs)
         n1_list = load_list("n1_list", n1)
         n2_list = load_list("n2_list", n2)
-        n3_list = load_list("n3_list", n3)
-        dw_table = load_words("dw_table", d_words, G)
-        cand_list = load_list("cand_list", cand)
-        xw_table = load_words("xw_table", x_words, T)
-        n4_list = load_list("n4_list", n4)
-        n5_list = load_list("n5_list", n5)
-        gs_raw = keep.tile([P, PACK], F32, name="gs_raw")
-        nc.gpsimd.dma_start(gs_raw[:], gs.rearrange("(p t) o -> p (t o)", t=PACK))
+        gain = keep.tile([P, PACK], F32, name="gain")
+        nc.gpsimd.dma_start(gain[:], gs.rearrange("(p t) o -> p (t o)", t=PACK))
         first_plane = zeroed_plane("first_plane", H + S)
         cand_plane = zeroed_plane("cand_plane", C)
 
-        gain = keep.tile([P, PACK], F32, name="gain")
-        nc.scalar.activation(out=gain[:], in_=gs_raw[:], func=COPY, scale=0.0625)
-
         first_picked = keep.tile([P, H + S], U8, name="first_picked", align_bytes=64)
-        nc.vector.tensor_copy(out=first_picked[:, H:], in_=xs_table[:].indirect(offs_list[:]))
         nc.vector.tensor_copy(out=first_picked[:, :H], in_=ds_table[:].indirect(k1_list[:]))
-        place_scale_rows(first_plane, first_picked, nc.scalar)
+        nc.vector.tensor_copy(out=first_picked[:, H:], in_=xs_table[:].indirect(offs_list[:]))
+        place_scale_rows(first_plane, first_picked, (nc.sync, nc.scalar))
+        n3_list = load_list("n3_list", n3)
+        cand_list = load_list("cand_list", cand)
+        n4_list = load_list("n4_list", n4)
+        n5_list = load_list("n5_list", n5)
 
         dw_picked = keep.tile([P, H], U32, name="dw_picked", tag="ds_table", align_bytes=64)
         nc.vector.tensor_copy(out=dw_picked[:], in_=dw_table[:].indirect(k1_list[:]))
@@ -86,11 +87,14 @@ def tile_picked_hpqhhaarhsendtwo_none_p_kernel(
 
         dw_dealt = keep.tile([P, PACK, P], U32, name="dw_dealt", align_bytes=64)
         ds_dealt = keep.tile([P, PACK, P], U8, name="ds_dealt", align_bytes=64)
-        dw_by_slot = dw_picked[:].rearrange("p (m t) -> p t m", t=PACK)
-        ds_by_slot = first_plane[:, :H].rearrange("p (m t) -> p t m", t=PACK)
+        nc.vector.tensor_copy(
+            out=dw_dealt[:].rearrange("p t (c i) -> p c t i", i=4),
+            in_=dw_picked[:].rearrange("p (c i t) -> p c t i", i=4, t=PACK),
+        )
+        ds_to = ds_dealt[:].rearrange("p t (c i) -> p c t i", i=16)
+        ds_from = first_plane[:, :H].rearrange("p (c i t) -> p c t i", i=16, t=PACK)
         for slots in (slice(0, 1), slice(1, PACK)):
-            nc.vector.tensor_copy(out=dw_dealt[:, slots, :], in_=dw_by_slot[:, slots, :])
-            nc.vector.tensor_copy(out=ds_dealt[:, slots, :], in_=ds_by_slot[:, slots, :])
+            nc.vector.tensor_copy(out=ds_to[:, :, slots, :], in_=ds_from[:, :, slots, :])
 
         h_rows = []
         for t in range(PACK):
@@ -106,14 +110,13 @@ def tile_picked_hpqhhaarhsendtwo_none_p_kernel(
             )
             h = keep.tile([P, S], F32, name=f"h{t}")
             if t == 0:
-                nc.scalar.activation(out=h[:], in_=bank[:], func=COPY)
+                nc.scalar.activation(out=h[:], in_=bank[:], func=COPY, scale=0.0625)
             else:
-                nc.vector.tensor_copy(out=h[:], in_=bank[:])
+                nc.vector.tensor_scalar(out=h[:], in0=bank[:], scalar1=0.0625, scalar2=None, op0=ALU.mult)
             h_rows.append(h)
 
         mixed = [None] * PACK
         dt_rows = [keep.tile([P, S], F32, name=f"dt{t}") for t in range(PACK)]
-        z_halves = [keep.tile([P, HALF, PACK], BF16, name=f"z_half{u}", align_bytes=64) for u in range(2)]
 
         def fetch_pairs(t):
             pair = keep.tile([P, 2, W], F32, name=f"pair{t}", align_bytes=64)
@@ -129,97 +132,109 @@ def tile_picked_hpqhhaarhsendtwo_none_p_kernel(
                 for t in ts:
                     nc.scalar.activation(out=dt_rows[t][:].indirect(places[:]), in_=mixed[t][:, side, :], func=COPY)
 
-        def make_z(t, u, other):
+        def larger_of(t, cols, other, larger):
             nc.scalar.activation(
-                out=other, in_=dt_rows[t][:].indirect(n3_list[:, 8 * u:8 * (u + 1)]), func=COPY
+                out=other, in_=dt_rows[t][:].indirect(n3_list[:, cols.start // 16:cols.stop // 16]), func=COPY
             )
-            larger = keep.tile([P, HALF], F32, name=f"larger{t}_{u}")
-            nc.vector.tensor_tensor(out=larger[:], in0=other, in1=dt_rows[t][:, HALF * u:HALF * (u + 1)], op=ALU.max)
-            nc.vector.tensor_scalar(
-                out=z_halves[u][:, :, t], in0=larger[:], scalar1=gain[:, t:t + 1], scalar2=None, op0=ALU.mult
-            )
+            nc.vector.tensor_tensor(out=larger, in0=other, in1=dt_rows[t][:, cols], op=ALU.max)
 
-        z_words = keep.tile([P, S], U32, name="z_words", align_bytes=64)
+        def weigh(t, larger, z):
+            nc.vector.tensor_scalar(out=z, in0=larger, scalar1=gain[:, t:t + 1], scalar2=None, op0=ALU.mult)
+
         z_plane = zeroed_plane("z_plane", S)
+        z_words = {}
 
-        def quantise_half(u):
-            cols = slice(HALF * u, HALF * (u + 1))
+        def quantise(cols, z):
+            words = keep.tile([P, cols.stop - cols.start], U32, name=f"z_words{cols.start}", align_bytes=64)
             nc.vector.quantize_mx(
-                out=z_words[:, cols].bitcast(FP8X4),
-                scales=z_plane[:, cols],
-                in_=z_halves[u][:].rearrange("p j t -> p (j t)"),
+                out=words[:].bitcast(FP8X4), scales=z_plane[:, cols], in_=z.rearrange("p j t -> p (j t)")
             )
+            z_words[cols.start] = words
 
-        early_other = keep.tile([P, PACK, HALF], F32, name="early_other")
+        early = slice(0, EARLY)
+        late = slice(EARLY, S)
+        late_parts = (slice(EARLY, 2 * EARLY), slice(2 * EARLY, S))
+        early_other = keep.tile([P, PACK, EARLY], F32, name="early_other")
+        early_larger = keep.tile([P, PACK, EARLY], F32, name="early_larger")
+        early_z = keep.tile([P, EARLY, PACK], BF16, name="early_z", align_bytes=64)
+
+        def make_early_z(t):
+            larger_of(t, early, early_other[:, t, :], early_larger[:, t, :])
+            weigh(t, early_larger[:, t, :], early_z[:, :, t])
+
         fetch_pairs(0)
         fetch_pairs(1)
-        cand_picked = keep.tile([P, C], U8, name="cand_picked", tag="pair0", align_bytes=64)
+        cand_picked = keep.tile([P, C], U8, name="cand_picked", tag="pair1", align_bytes=64)
         nc.vector.tensor_copy(out=cand_picked[:], in_=xs_table[:].indirect(cand_list[:]))
-        place_scale_rows(cand_plane, cand_picked, nc.sync)
+        place_scale_rows(cand_plane, cand_picked, (nc.sync,))
         send_pairs((0, 1))
         fetch_pairs(2)
         fetch_pairs(3)
-        cand_words = keep.tile([P, C], U32, name="cand_words", tag="pair2", align_bytes=64)
+        cand_words = keep.tile([P, C], U32, name="cand_words", tag="pair3", align_bytes=64)
         nc.vector.tensor_copy(out=cand_words[:], in_=xw_table[:].indirect(cand_list[:]))
-        make_z(0, 0, early_other[:, 0, :])
-        make_z(1, 0, early_other[:, 1, :])
+        make_early_z(0)
+        make_early_z(1)
         send_pairs((2, 3))
-        make_z(2, 0, early_other[:, 2, :])
-        make_z(3, 0, early_other[:, 3, :])
-        quantise_half(0)
+        make_early_z(2)
+        make_early_z(3)
+        quantise(early, early_z[:])
 
         scores = [keep.tile([P, S], F32, name=f"scores{c}") for c in range(C // P)]
 
-        def score(c, cols, bank_tag):
-            width = cols.stop - cols.start
-            bank = psum.tile([P, width], F32, name=f"s_bank{c}_{cols.start}", tag=bank_tag)
-            nc.tensor.matmul_mx(
-                out=bank[:],
-                lhsT=cand_words[:, P * c:P * (c + 1)].bitcast(FP8X4),
-                lhsT_scale=cand_plane[:, P * c:P * (c + 1)],
-                rhs=z_words[:, cols].bitcast(FP8X4),
-                rhs_scale=z_plane[:, cols],
-                start=True,
-                stop=True,
+        def score(c, parts, bank_tag):
+            first, last = parts[0].start, parts[-1].stop
+            bank = psum.tile([P, last - first], F32, name=f"s_bank{c}_{first}", tag=bank_tag)
+            for cols in parts:
+                nc.tensor.matmul_mx(
+                    out=bank[:, cols.start - first:cols.stop - first],
+                    lhsT=cand_words[:, P * c:P * (c + 1)].bitcast(FP8X4),
+                    lhsT_scale=cand_plane[:, P * c:P * (c + 1)],
+                    rhs=z_words[cols.start][:].bitcast(FP8X4),
+                    rhs_scale=z_plane[:, cols],
+                    start=True,
+                    stop=True,
+                )
+            nc.vector.tensor_scalar(
+                out=scores[c][:, first:last], in0=bank[:], scalar1=0.0625, scalar2=None, op0=ALU.mult
             )
-            nc.vector.tensor_scalar(out=scores[c][:, cols], in0=bank[:], scalar1=0.0625, scalar2=None, op0=ALU.mult)
 
-        sent = {}
-        for c in range(C // P):
-            width = S if c < SPLIT_BLOCKS else 2 * S
-            for side in range(2):
-                sent[c, side] = keep.tile([P, width], F32, name=f"sent{c}_{side}")
+        sent = [[keep.tile([P, S], F32, name=f"sent{c}_{side}") for side in range(2)] for c in range(C // P)]
 
         def send_scores(c, cols):
             for side, places in enumerate((n4_list, n5_list)):
                 nc.scalar.activation(
-                    out=sent[c, side][:].indirect(places[:, cols.start // 16:cols.stop // 16]),
+                    out=sent[c][side][:].indirect(places[:, cols.start // 16:cols.stop // 16]),
                     in_=scores[c][:, cols],
                     func=COPY,
                 )
 
-        def finish(c):
-            result = keep.tile([P, S], F32, name=f"result{c}")
-            nc.vector.tensor_tensor(out=result[:], in0=sent[c, 0][:, :S], in1=sent[c, 1][:, :S], op=ALU.max)
-            nc.sync.dma_start(out[P * c:P * (c + 1), :], result[:])
+        for c in range(C // P):
+            score(c, (early,), f"bank{c}")
 
-        for c in range(SPLIT_BLOCKS):
-            score(c, slice(0, HALF), f"bank{c}")
-
-        late_other = keep.tile([P, PACK, HALF], F32, name="late_other", tag="mix3")
+        late_other = keep.tile([P, PACK, LATE], F32, name="late_other", tag="mix3")
+        late_larger = [
+            keep.tile([P, 2, LATE], F32, name=f"late_larger{n}", tag=tag, align_bytes=64)
+            for n, tag in enumerate(("early_z", "z_words0"))
+        ]
+        late_rows = keep.tile([P, PACK, LATE], BF16, name="late_rows")
+        late_z = keep.tile([P, LATE, PACK], BF16, name="late_z", align_bytes=64)
         for t in range(PACK):
-            make_z(t, 1, late_other[:, t, :])
-        quantise_half(1)
+            larger = late_larger[t // 2][:, t % 2, :]
+            larger_of(t, late, late_other[:, t, :], larger)
+            weigh(t, larger, late_rows[:, t, :])
+        nc.vector.tensor_copy(
+            out=late_z[:].rearrange("p (c i) t -> p c t i", i=4),
+            in_=late_rows[:].rearrange("p t (c i) -> p c t i", i=4),
+        )
+        for cols in late_parts:
+            quantise(cols, late_z[:, cols.start - EARLY:cols.stop - EARLY, :])
 
-        for c in range(SPLIT_BLOCKS):
-            send_scores(c, slice(0, HALF))
-        for c in range(SPLIT_BLOCKS):
-            score(c, slice(HALF, S), f"bank{SPLIT_BLOCKS + c}")
-        for c in range(SPLIT_BLOCKS, C // P):
-            score(c, slice(0, S), f"bank{SPLIT_BLOCKS + c}")
-        for c in range(SPLIT_BLOCKS):
-            send_scores(c, slice(HALF, S))
-            finish(c)
-        for c in range(SPLIT_BLOCKS, C // P):
-            send_scores(c, slice(0, S))
-            finish(c)
+        for c in range(C // P):
+            send_scores(c, early)
+        for c in range(C // P):
+            score(c, late_parts, f"bank{PACK + c}")
+        for c in range(C // P):
+            send_scores(c, late)
+            result = keep.tile([P, S], F32, name=f"result{c}")
+            nc.vector.tensor_tensor(out=result[:], in0=sent[c][0][:], in1=sent[c][1][:], op=ALU.max)
+            nc.sync.dma_start(out[P * c:P * (c + 1), :], result[:])

@@ -43,7 +43,7 @@ def tile_picked_hpqhhaarhsendtwo_none_p_kernel(
             share = width // len(zeroers)
             for n, engine in enumerate(zeroers):
                 engine.memset(held[:, n * share:(n + 1) * share].bitcast(I32), 0)
-            nc.scalar.dma_start(held[0:P:8, :].bitcast(I32), dram[0].bitcast(I32))
+            nc.sync.dma_start(held[0:P:8, :].bitcast(I32), dram[0].bitcast(I32))
             return held
 
         def zeroed_plane(name, width):
@@ -55,17 +55,15 @@ def tile_picked_hpqhhaarhsendtwo_none_p_kernel(
             for i in range(4):
                 queues[i % len(queues)].dma_start(plane[i:P:32, :].bitcast(I32), picked[8 * i:P:32, :].bitcast(I32))
 
-        ds_table = load_scales("ds_table", d_scales, G, (nc.vector, nc.gpsimd))
-        xs_table = load_scales("xs_table", x_scales, T, (nc.vector,))
         dw_table = keep.tile([P, G], U32, name="dw_table", align_bytes=64)
         xw_table = keep.tile([P, T], U32, name="xw_table", align_bytes=64)
         load_words(nc.scalar, dw_table, d_words, slice(0, DW_FIRST))
-        load_words(nc.scalar, dw_table, d_words, slice(DW_FIRST, G))
-        load_words(nc.scalar, xw_table, x_words, slice(0, T))
+        ds_table = load_scales("ds_table", d_scales, G, (nc.vector, nc.gpsimd))
         k1_list = load_list("k1_list", k1)
         offs_list = load_list("offs_list", offs)
-        n1_list = load_list("n1_list", n1)
-        n2_list = load_list("n2_list", n2)
+        xs_table = load_scales("xs_table", x_scales, T, (nc.vector,))
+        load_words(nc.sync, dw_table, d_words, slice(DW_FIRST, G))
+        load_words(nc.sync, xw_table, x_words, slice(0, T))
         gain = keep.tile([P, PACK], F32, name="gain")
         nc.gpsimd.dma_start(gain[:], gs.rearrange("(p t) o -> p (t o)", t=PACK))
         first_plane = zeroed_plane("first_plane", H + S)
@@ -75,8 +73,10 @@ def tile_picked_hpqhhaarhsendtwo_none_p_kernel(
         nc.vector.tensor_copy(out=first_picked[:, :H], in_=ds_table[:].indirect(k1_list[:]))
         nc.vector.tensor_copy(out=first_picked[:, H:], in_=xs_table[:].indirect(offs_list[:]))
         place_scale_rows(first_plane, first_picked, (nc.sync, nc.scalar))
-        n3_list = load_list("n3_list", n3)
+        n1_list = load_list("n1_list", n1)
+        n2_list = load_list("n2_list", n2)
         cand_list = load_list("cand_list", cand)
+        n3_list = load_list("n3_list", n3)
         n4_list = load_list("n4_list", n4)
         n5_list = load_list("n5_list", n5)
 
@@ -115,22 +115,24 @@ def tile_picked_hpqhhaarhsendtwo_none_p_kernel(
                 nc.vector.tensor_scalar(out=h[:], in0=bank[:], scalar1=0.0625, scalar2=None, op0=ALU.mult)
             h_rows.append(h)
 
-        mixed = [None] * PACK
-        dt_rows = [keep.tile([P, S], F32, name=f"dt{t}") for t in range(PACK)]
+        mixed = {}
+        dt_rows = {}
 
         def fetch_pairs(t):
-            pair = keep.tile([P, 2, W], F32, name=f"pair{t}", align_bytes=64)
-            nc.scalar.activation(out=pair[:, 0, :], in_=h_rows[t][:].indirect(n1_list[:]), func=COPY)
-            nc.scalar.activation(out=pair[:, 1, :], in_=h_rows[t][:].indirect(n2_list[:]), func=COPY)
-            mix = keep.tile([P, 2, W], F32, name=f"mix{t}")
-            nc.vector.tensor_tensor(out=mix[:, 0, :], in0=pair[:, 0, :], in1=pair[:, 1, :], op=ALU.add)
-            nc.vector.tensor_tensor(out=mix[:, 1, :], in0=pair[:, 0, :], in1=pair[:, 1, :], op=ALU.subtract)
-            mixed[t] = mix
+            pa = keep.tile([P, W], F32, name=f"pa{t}", align_bytes=64)
+            pb = keep.tile([P, W], F32, name=f"pb{t}", align_bytes=64)
+            nc.scalar.activation(out=pa[:], in_=h_rows[t][:].indirect(n1_list[:]), func=COPY)
+            nc.scalar.activation(out=pb[:], in_=h_rows[t][:].indirect(n2_list[:]), func=COPY)
+            for side, op in enumerate((ALU.add, ALU.subtract)):
+                mixed[t, side] = keep.tile([P, W], F32, name=f"mix{t}_{side}")
+                nc.vector.tensor_tensor(out=mixed[t, side][:], in0=pa[:], in1=pb[:], op=op)
 
-        def send_pairs(ts):
-            for side, places in enumerate((n1_list, n2_list)):
-                for t in ts:
-                    nc.scalar.activation(out=dt_rows[t][:].indirect(places[:]), in_=mixed[t][:, side, :], func=COPY)
+        def send_pair(t, side):
+            if side == 0:
+                tag = f"dt{t}" if t < 2 else f"mix{t - 2}_1"
+                dt_rows[t] = keep.tile([P, S], F32, name=f"dt{t}", tag=tag)
+            places = (n1_list, n2_list)[side]
+            nc.scalar.activation(out=dt_rows[t][:].indirect(places[:]), in_=mixed[t, side][:], func=COPY)
 
         def larger_of(t, cols, other, larger):
             nc.scalar.activation(
@@ -154,29 +156,36 @@ def tile_picked_hpqhhaarhsendtwo_none_p_kernel(
         early = slice(0, EARLY)
         late = slice(EARLY, S)
         late_parts = (slice(EARLY, 2 * EARLY), slice(2 * EARLY, S))
-        early_other = keep.tile([P, PACK, EARLY], F32, name="early_other")
-        early_larger = keep.tile([P, PACK, EARLY], F32, name="early_larger")
         early_z = keep.tile([P, EARLY, PACK], BF16, name="early_z", align_bytes=64)
 
-        def make_early_z(t):
-            larger_of(t, early, early_other[:, t, :], early_larger[:, t, :])
-            weigh(t, early_larger[:, t, :], early_z[:, :, t])
+        def make_early_z(ts):
+            larger = {}
+            for t in ts:
+                other = keep.tile([P, EARLY], F32, name=f"early_other{t}")
+                larger[t] = keep.tile([P, EARLY], F32, name=f"early_larger{t}")
+                larger_of(t, early, other[:], larger[t][:])
+            for t in ts:
+                weigh(t, larger[t][:], early_z[:, :, t])
 
         fetch_pairs(0)
         fetch_pairs(1)
-        cand_picked = keep.tile([P, C], U8, name="cand_picked", tag="pair1", align_bytes=64)
+        cand_picked = keep.tile([P, C], U8, name="cand_picked", tag="pb1", align_bytes=64)
         nc.vector.tensor_copy(out=cand_picked[:], in_=xs_table[:].indirect(cand_list[:]))
         place_scale_rows(cand_plane, cand_picked, (nc.sync,))
-        send_pairs((0, 1))
+        for side in range(2):
+            send_pair(0, side)
+            send_pair(1, side)
         fetch_pairs(2)
-        fetch_pairs(3)
-        cand_words = keep.tile([P, C], U32, name="cand_words", tag="pair3", align_bytes=64)
+        cand_words = keep.tile([P, C], U32, name="cand_words", tag="pb2", align_bytes=64)
         nc.vector.tensor_copy(out=cand_words[:], in_=xw_table[:].indirect(cand_list[:]))
-        make_early_z(0)
-        make_early_z(1)
-        send_pairs((2, 3))
-        make_early_z(2)
-        make_early_z(3)
+        fetch_pairs(3)
+        make_early_z((0,))
+        send_pair(2, 0)
+        make_early_z((1,))
+        send_pair(3, 0)
+        send_pair(2, 1)
+        send_pair(3, 1)
+        make_early_z((2, 3))
         quantise(early, early_z[:])
 
         scores = [keep.tile([P, S], F32, name=f"scores{c}") for c in range(C // P)]
@@ -194,9 +203,12 @@ def tile_picked_hpqhhaarhsendtwo_none_p_kernel(
                     start=True,
                     stop=True,
                 )
-            nc.vector.tensor_scalar(
-                out=scores[c][:, first:last], in0=bank[:], scalar1=0.0625, scalar2=None, op0=ALU.mult
-            )
+            if first == 0 and c < 2:
+                nc.scalar.activation(out=scores[c][:, first:last], in_=bank[:], func=COPY, scale=0.0625)
+            else:
+                nc.vector.tensor_scalar(
+                    out=scores[c][:, first:last], in0=bank[:], scalar1=0.0625, scalar2=None, op0=ALU.mult
+                )
 
         sent = [[keep.tile([P, S], F32, name=f"sent{c}_{side}") for side in range(2)] for c in range(C // P)]
 
@@ -211,15 +223,12 @@ def tile_picked_hpqhhaarhsendtwo_none_p_kernel(
         for c in range(C // P):
             score(c, (early,), f"bank{c}")
 
-        late_other = keep.tile([P, PACK, LATE], F32, name="late_other", tag="mix3")
-        late_larger = [
-            keep.tile([P, 2, LATE], F32, name=f"late_larger{n}", tag=tag, align_bytes=64)
-            for n, tag in enumerate(("early_z", "z_words0"))
-        ]
+        late_other = keep.tile([P, PACK, LATE], F32, name="late_other", tag="early_other3")
+        late_larger = keep.tile([P, PACK, LATE], F32, name="late_larger", tag="early_z", align_bytes=64)
         late_rows = keep.tile([P, PACK, LATE], BF16, name="late_rows")
-        late_z = keep.tile([P, LATE, PACK], BF16, name="late_z", align_bytes=64)
+        late_z = keep.tile([P, LATE, PACK], BF16, name="late_z", tag="z_words0", align_bytes=64)
         for t in range(PACK):
-            larger = late_larger[t // 2][:, t % 2, :]
+            larger = late_larger[:, t, :]
             larger_of(t, late, late_other[:, t, :], larger)
             weigh(t, larger, late_rows[:, t, :])
         nc.vector.tensor_copy(
@@ -232,7 +241,7 @@ def tile_picked_hpqhhaarhsendtwo_none_p_kernel(
         for c in range(C // P):
             send_scores(c, early)
         for c in range(C // P):
-            score(c, late_parts, f"bank{PACK + c}")
+            score(c, late_parts, "late_bank")
         for c in range(C // P):
             send_scores(c, late)
             result = keep.tile([P, S], F32, name=f"result{c}")

@@ -58,7 +58,7 @@ def tile_picked_hpqhhaarhsendtwo_none_p_kernel(
         dw_table = keep.tile([P, G], U32, name="dw_table", align_bytes=64)
         xw_table = keep.tile([P, T], U32, name="xw_table", align_bytes=64)
         load_words(nc.scalar, dw_table, d_words, slice(0, DW_FIRST))
-        ds_table = load_scales("ds_table", d_scales, G, (nc.vector, nc.gpsimd))
+        ds_table = load_scales("ds_table", d_scales, G, (nc.vector,))
         k1_list = load_list("k1_list", k1)
         offs_list = load_list("offs_list", offs)
         xs_table = load_scales("xs_table", x_scales, T, (nc.vector,))
@@ -82,26 +82,26 @@ def tile_picked_hpqhhaarhsendtwo_none_p_kernel(
 
         dw_picked = keep.tile([P, H], U32, name="dw_picked", tag="ds_table", align_bytes=64)
         nc.vector.tensor_copy(out=dw_picked[:], in_=dw_table[:].indirect(k1_list[:]))
+        dw_from = dw_picked[:].rearrange("p (c i t) -> p c t i", i=4, t=PACK)
+        ds_from = first_plane[:, :H].rearrange("p (c i t) -> p c t i", i=16, t=PACK)
+        dw_first = keep.tile([P, 1, P], U32, name="dw_first", align_bytes=64)
+        nc.vector.tensor_copy(out=dw_first[:].rearrange("p t (c i) -> p c t i", i=4), in_=dw_from[:, :, 0:1, :])
         xq_words = keep.tile([P, S], U32, name="xq_words", align_bytes=64)
         nc.vector.tensor_copy(out=xq_words[:], in_=xw_table[:].indirect(offs_list[:]))
-
-        dw_dealt = keep.tile([P, PACK, P], U32, name="dw_dealt", align_bytes=64)
         ds_dealt = keep.tile([P, PACK, P], U8, name="ds_dealt", align_bytes=64)
-        nc.vector.tensor_copy(
-            out=dw_dealt[:].rearrange("p t (c i) -> p c t i", i=4),
-            in_=dw_picked[:].rearrange("p (c i t) -> p c t i", i=4, t=PACK),
-        )
         ds_to = ds_dealt[:].rearrange("p t (c i) -> p c t i", i=16)
-        ds_from = first_plane[:, :H].rearrange("p (c i t) -> p c t i", i=16, t=PACK)
-        for slots in (slice(0, 1), slice(1, PACK)):
-            nc.vector.tensor_copy(out=ds_to[:, :, slots, :], in_=ds_from[:, :, slots, :])
+        nc.vector.tensor_copy(out=ds_to[:, :, 0:1, :], in_=ds_from[:, :, 0:1, :])
+        dw_rest = keep.tile([P, PACK - 1, P], U32, name="dw_rest", tag="first_picked", align_bytes=64)
+        nc.vector.tensor_copy(out=dw_rest[:].rearrange("p t (c i) -> p c t i", i=4), in_=dw_from[:, :, 1:PACK, :])
+        nc.vector.tensor_copy(out=ds_to[:, :, 1:PACK, :], in_=ds_from[:, :, 1:PACK, :])
+        dw_dealt = [dw_first[:, 0, :]] + [dw_rest[:, t, :] for t in range(PACK - 1)]
 
         h_rows = []
         for t in range(PACK):
             bank = psum.tile([P, S], F32, name=f"h_bank{t}", tag=f"bank{t}")
             nc.tensor.matmul_mx(
                 out=bank[:],
-                lhsT=dw_dealt[:, t, :].bitcast(FP8X4),
+                lhsT=dw_dealt[t].bitcast(FP8X4),
                 lhsT_scale=ds_dealt[:, t, :],
                 rhs=xq_words[:].bitcast(FP8X4),
                 rhs_scale=first_plane[:, H:],

@@ -17,9 +17,15 @@ COPY = mybir.ActivationFunctionType.Copy
 
 P = 128
 PACK = 4
+BLOCK_PARTITIONS = 8
+QUADRANT = 32
+LIST_ROWS = 16
+BLOCKS = C // P
+SIXTEENTH = 0.0625
 EARLY = 64
 LATE = S - EARLY
 DW_FIRST = G // 4
+SCALAR_EMPTIES = 2
 
 
 def tile_picked_hpqhhaarhsendtwo_none_p_kernel(
@@ -35,69 +41,70 @@ def tile_picked_hpqhhaarhsendtwo_none_p_kernel(
             nc.sync.dma_start(held[:], dram)
             return held
 
-        def load_words(queue, held, dram, cols):
-            queue.dma_start(held[:, cols].bitcast(I32), dram[0].rearrange("p n t -> p (n t)").bitcast(I32)[:, cols])
+        def load_words(queue, table, dram, cols):
+            queue.dma_start(table[:, cols].bitcast(I32), dram[0].rearrange("p n t -> p (n t)").bitcast(I32)[:, cols])
 
-        def load_scales(name, dram, width, zeroers):
+        def zeroed_bytes(name, width):
             held = keep.tile([P, width], U8, name=name, align_bytes=64)
-            share = width // len(zeroers)
-            for n, engine in enumerate(zeroers):
-                engine.memset(held[:, n * share:(n + 1) * share].bitcast(I32), 0)
-            nc.sync.dma_start(held[0:P:8, :].bitcast(I32), dram[0].bitcast(I32))
+            nc.vector.memset(held[:].bitcast(I32), 0)
             return held
 
-        def zeroed_plane(name, width):
-            plane = keep.tile([P, width], U8, name=name, align_bytes=64)
-            nc.vector.memset(plane[:].bitcast(I32), 0)
-            return plane
+        def load_scales(name, dram, width):
+            table = zeroed_bytes(name, width)
+            nc.sync.dma_start(table[0:P:BLOCK_PARTITIONS, :].bitcast(I32), dram[0].bitcast(I32))
+            return table
 
         def place_scale_rows(plane, picked, queues):
-            for i in range(4):
-                queues[i % len(queues)].dma_start(plane[i:P:32, :].bitcast(I32), picked[8 * i:P:32, :].bitcast(I32))
+            for i in range(QUADRANT // BLOCK_PARTITIONS):
+                queues[i % len(queues)].dma_start(
+                    plane[i:P:QUADRANT, :].bitcast(I32), picked[BLOCK_PARTITIONS * i:P:QUADRANT, :].bitcast(I32)
+                )
+
+        def entries(held, cols):
+            return held[:, cols.start // LIST_ROWS:cols.stop // LIST_ROWS]
 
         dw_table = keep.tile([P, G], U32, name="dw_table", align_bytes=64)
         xw_table = keep.tile([P, T], U32, name="xw_table", align_bytes=64)
         load_words(nc.scalar, dw_table, d_words, slice(0, DW_FIRST))
-        ds_table = load_scales("ds_table", d_scales, G, (nc.vector,))
-        k1_list = load_list("k1_list", k1)
+        xs_table = load_scales("xs_table", x_scales, T)
         offs_list = load_list("offs_list", offs)
-        xs_table = load_scales("xs_table", x_scales, T, (nc.vector,))
+        k1_list = load_list("k1_list", k1)
+        ds_table = load_scales("ds_table", d_scales, G)
         load_words(nc.sync, dw_table, d_words, slice(DW_FIRST, G))
         load_words(nc.sync, xw_table, x_words, slice(0, T))
-        gain = keep.tile([P, PACK], F32, name="gain")
-        nc.gpsimd.dma_start(gain[:], gs.rearrange("(p t) o -> p (t o)", t=PACK))
-        first_plane = zeroed_plane("first_plane", H + S)
-        cand_plane = zeroed_plane("cand_plane", C)
+        first_plane = zeroed_bytes("first_plane", H + S)
+        cand_plane = zeroed_bytes("cand_plane", C)
 
         first_picked = keep.tile([P, H + S], U8, name="first_picked", align_bytes=64)
-        nc.vector.tensor_copy(out=first_picked[:, :H], in_=ds_table[:].indirect(k1_list[:]))
         nc.vector.tensor_copy(out=first_picked[:, H:], in_=xs_table[:].indirect(offs_list[:]))
+        nc.vector.tensor_copy(out=first_picked[:, :H], in_=ds_table[:].indirect(k1_list[:]))
         place_scale_rows(first_plane, first_picked, (nc.sync, nc.scalar))
         n1_list = load_list("n1_list", n1)
         n2_list = load_list("n2_list", n2)
         cand_list = load_list("cand_list", cand)
         n3_list = load_list("n3_list", n3)
+        gain = keep.tile([P, PACK], F32, name="gain")
+        nc.sync.dma_start(gain[:], gs.rearrange("(p t) o -> p (t o)", t=PACK))
         n4_list = load_list("n4_list", n4)
         n5_list = load_list("n5_list", n5)
 
         dw_picked = keep.tile([P, H], U32, name="dw_picked", tag="ds_table", align_bytes=64)
         nc.vector.tensor_copy(out=dw_picked[:], in_=dw_table[:].indirect(k1_list[:]))
-        dw_from = dw_picked[:].rearrange("p (c i t) -> p c t i", i=4, t=PACK)
-        ds_from = first_plane[:, :H].rearrange("p (c i t) -> p c t i", i=16, t=PACK)
-        dw_first = keep.tile([P, 1, P], U32, name="dw_first", align_bytes=64)
-        nc.vector.tensor_copy(out=dw_first[:].rearrange("p t (c i) -> p c t i", i=4), in_=dw_from[:, :, 0:1, :])
+        dw_by_slot = dw_picked[:].rearrange("p (m t) -> p t m", t=PACK)
+        ds_by_slot = first_plane[:, :H].rearrange("p (m t) -> p t m", t=PACK)
+        dw_first = keep.tile([P, P], U32, name="dw_first", align_bytes=64)
+        nc.vector.tensor_copy(out=dw_first[:], in_=dw_by_slot[:, 0, :])
         xq_words = keep.tile([P, S], U32, name="xq_words", align_bytes=64)
         nc.vector.tensor_copy(out=xq_words[:], in_=xw_table[:].indirect(offs_list[:]))
         ds_dealt = keep.tile([P, PACK, P], U8, name="ds_dealt", align_bytes=64)
-        ds_to = ds_dealt[:].rearrange("p t (c i) -> p c t i", i=16)
-        nc.vector.tensor_copy(out=ds_to[:, :, 0:1, :], in_=ds_from[:, :, 0:1, :])
         dw_rest = keep.tile([P, PACK - 1, P], U32, name="dw_rest", tag="first_picked", align_bytes=64)
-        nc.vector.tensor_copy(out=dw_rest[:].rearrange("p t (c i) -> p c t i", i=4), in_=dw_from[:, :, 1:PACK, :])
-        nc.vector.tensor_copy(out=ds_to[:, :, 1:PACK, :], in_=ds_from[:, :, 1:PACK, :])
-        dw_dealt = [dw_first[:, 0, :]] + [dw_rest[:, t, :] for t in range(PACK - 1)]
+        dw_dealt = [dw_first[:]] + [dw_rest[:, t, :] for t in range(PACK - 1)]
 
         h_rows = []
         for t in range(PACK):
+            nc.vector.tensor_copy(out=ds_dealt[:, t, :], in_=ds_by_slot[:, t, :])
+            if t > 0:
+                nc.vector.tensor_copy(out=dw_dealt[t], in_=dw_by_slot[:, t, :])
             bank = psum.tile([P, S], F32, name=f"h_bank{t}", tag=f"bank{t}")
             nc.tensor.matmul_mx(
                 out=bank[:],
@@ -110,9 +117,9 @@ def tile_picked_hpqhhaarhsendtwo_none_p_kernel(
             )
             h = keep.tile([P, S], F32, name=f"h{t}")
             if t == 0:
-                nc.scalar.activation(out=h[:], in_=bank[:], func=COPY, scale=0.0625)
+                nc.scalar.activation(out=h[:], in_=bank[:], func=COPY, scale=SIXTEENTH)
             else:
-                nc.vector.tensor_scalar(out=h[:], in0=bank[:], scalar1=0.0625, scalar2=None, op0=ALU.mult)
+                nc.vector.tensor_scalar(out=h[:], in0=bank[:], scalar1=SIXTEENTH, scalar2=None, op0=ALU.mult)
             h_rows.append(h)
 
         mixed = {}
@@ -135,15 +142,13 @@ def tile_picked_hpqhhaarhsendtwo_none_p_kernel(
             nc.scalar.activation(out=dt_rows[t][:].indirect(places[:]), in_=mixed[t, side][:], func=COPY)
 
         def larger_of(t, cols, other, larger):
-            nc.scalar.activation(
-                out=other, in_=dt_rows[t][:].indirect(n3_list[:, cols.start // 16:cols.stop // 16]), func=COPY
-            )
+            nc.scalar.activation(out=other, in_=dt_rows[t][:].indirect(entries(n3_list, cols)), func=COPY)
             nc.vector.tensor_tensor(out=larger, in0=other, in1=dt_rows[t][:, cols], op=ALU.max)
 
         def weigh(t, larger, z):
             nc.vector.tensor_scalar(out=z, in0=larger, scalar1=gain[:, t:t + 1], scalar2=None, op0=ALU.mult)
 
-        z_plane = zeroed_plane("z_plane", S)
+        z_plane = keep.tile([P, S], U8, name="z_plane", align_bytes=64)
         z_words = {}
 
         def quantise(cols, z):
@@ -158,13 +163,13 @@ def tile_picked_hpqhhaarhsendtwo_none_p_kernel(
         late_parts = (slice(EARLY, 2 * EARLY), slice(2 * EARLY, S))
         early_z = keep.tile([P, EARLY, PACK], BF16, name="early_z", align_bytes=64)
 
-        def make_early_z(ts):
+        def make_early_z(slots):
             larger = {}
-            for t in ts:
+            for t in slots:
                 other = keep.tile([P, EARLY], F32, name=f"early_other{t}")
                 larger[t] = keep.tile([P, EARLY], F32, name=f"early_larger{t}")
                 larger_of(t, early, other[:], larger[t][:])
-            for t in ts:
+            for t in slots:
                 weigh(t, larger[t][:], early_z[:, :, t])
 
         fetch_pairs(0)
@@ -188,9 +193,9 @@ def tile_picked_hpqhhaarhsendtwo_none_p_kernel(
         make_early_z((2, 3))
         quantise(early, early_z[:])
 
-        scores = [keep.tile([P, S], F32, name=f"scores{c}") for c in range(C // P)]
+        scores = [keep.tile([P, S], F32, name=f"scores{c}") for c in range(BLOCKS)]
 
-        def score(c, parts, bank_tag):
+        def score(c, parts, bank_tag, on_scalar):
             first, last = parts[0].start, parts[-1].stop
             bank = psum.tile([P, last - first], F32, name=f"s_bank{c}_{first}", tag=bank_tag)
             for cols in parts:
@@ -203,34 +208,31 @@ def tile_picked_hpqhhaarhsendtwo_none_p_kernel(
                     start=True,
                     stop=True,
                 )
-            if first == 0 and c < 2:
-                nc.scalar.activation(out=scores[c][:, first:last], in_=bank[:], func=COPY, scale=0.0625)
+            if on_scalar:
+                nc.scalar.activation(out=scores[c][:, first:last], in_=bank[:], func=COPY, scale=SIXTEENTH)
             else:
                 nc.vector.tensor_scalar(
-                    out=scores[c][:, first:last], in0=bank[:], scalar1=0.0625, scalar2=None, op0=ALU.mult
+                    out=scores[c][:, first:last], in0=bank[:], scalar1=SIXTEENTH, scalar2=None, op0=ALU.mult
                 )
 
-        sent = [[keep.tile([P, S], F32, name=f"sent{c}_{side}") for side in range(2)] for c in range(C // P)]
+        sent = [[keep.tile([P, S], F32, name=f"sent{c}_{side}") for side in range(2)] for c in range(BLOCKS)]
 
         def send_scores(c, cols):
             for side, places in enumerate((n4_list, n5_list)):
                 nc.scalar.activation(
-                    out=sent[c][side][:].indirect(places[:, cols.start // 16:cols.stop // 16]),
-                    in_=scores[c][:, cols],
-                    func=COPY,
+                    out=sent[c][side][:].indirect(entries(places, cols)), in_=scores[c][:, cols], func=COPY
                 )
 
-        for c in range(C // P):
-            score(c, (early,), f"bank{c}")
+        for c in range(BLOCKS):
+            score(c, (early,), f"bank{c}", c < SCALAR_EMPTIES)
 
-        late_other = keep.tile([P, PACK, LATE], F32, name="late_other", tag="early_other3")
+        late_other = keep.tile([P, PACK, LATE], F32, name="late_other", tag=f"early_other{PACK - 1}")
         late_larger = keep.tile([P, PACK, LATE], F32, name="late_larger", tag="early_z", align_bytes=64)
         late_rows = keep.tile([P, PACK, LATE], BF16, name="late_rows")
-        late_z = keep.tile([P, LATE, PACK], BF16, name="late_z", tag="z_words0", align_bytes=64)
+        late_z = keep.tile([P, LATE, PACK], BF16, name="late_z", tag=f"z_words{early.start}", align_bytes=64)
         for t in range(PACK):
-            larger = late_larger[:, t, :]
-            larger_of(t, late, late_other[:, t, :], larger)
-            weigh(t, larger, late_rows[:, t, :])
+            larger_of(t, late, late_other[:, t, :], late_larger[:, t, :])
+            weigh(t, late_larger[:, t, :], late_rows[:, t, :])
         nc.vector.tensor_copy(
             out=late_z[:].rearrange("p (c i) t -> p c t i", i=4),
             in_=late_rows[:].rearrange("p t (c i) -> p c t i", i=4),
@@ -238,11 +240,11 @@ def tile_picked_hpqhhaarhsendtwo_none_p_kernel(
         for cols in late_parts:
             quantise(cols, late_z[:, cols.start - EARLY:cols.stop - EARLY, :])
 
-        for c in range(C // P):
+        for c in range(BLOCKS):
             send_scores(c, early)
-        for c in range(C // P):
-            score(c, late_parts, "late_bank")
-        for c in range(C // P):
+        for c in range(BLOCKS):
+            score(c, late_parts, "late_bank", False)
+        for c in range(BLOCKS):
             send_scores(c, late)
             result = keep.tile([P, S], F32, name=f"result{c}")
             nc.vector.tensor_tensor(out=result[:], in0=sent[c][0][:], in1=sent[c][1][:], op=ALU.max)

from contextlib import ExitStack

import concourse.mybir as mybir

K, T, S, G, H, W, C = 512, 1024, 256, 2048, 512, 128, 512
FLOPS = 2 * K * H * S + 2 * K * C * S

F32 = mybir.dt.float32
BF16 = mybir.dt.bfloat16
I32 = mybir.dt.int32
U32 = mybir.dt.uint32
U16 = mybir.dt.uint16
U8 = mybir.dt.uint8
FP8X4 = mybir.dt.float8_e4m3fn_x4
ALU = mybir.AluOpType
COPY = mybir.ActivationFunctionType.Copy

P = 128
PACK = 4
BLOCK_PARTITIONS = 8
QUADRANT = 32
LIST_ROWS = 16
BLOCKS = C // P
SIXTEENTH = 0.0625
EARLY = 64
LATE = S - EARLY
DW_FIRST = G // 4
SCALAR_EMPTIES = 2


def tile_picked_hpqhhaarhsendtwo_none_p_kernel(
    tc, x_words, x_scales, d_words, d_scales, gs, offs, k1, n1, n2, n3, cand, n4, n5, out
):
    nc = tc.nc
    with ExitStack() as ctx:
        keep = ctx.enter_context(tc.tile_pool(name="keep", bufs=1))
        psum = ctx.enter_context(tc.psum_pool(name="psum", bufs=1))

        def load_list(name, dram):
            held = keep.tile(list(dram.shape), U16, name=name)
            nc.sync.dma_start(held[:], dram)
            return held

        def load_words(queue, table, dram, cols):
            queue.dma_start(table[:, cols].bitcast(I32), dram[0].rearrange("p n t -> p (n t)").bitcast(I32)[:, cols])

        def zeroed_bytes(name, width):
            held = keep.tile([P, width], U8, name=name, align_bytes=64)
            nc.vector.memset(held[:].bitcast(I32), 0)
            return held

        def load_scales(name, dram, width):
            table = zeroed_bytes(name, width)
            nc.sync.dma_start(table[0:P:BLOCK_PARTITIONS, :].bitcast(I32), dram[0].bitcast(I32))
            return table

        def place_scale_rows(plane, picked, queues):
            for i in range(QUADRANT // BLOCK_PARTITIONS):
                queues[i % len(queues)].dma_start(
                    plane[i:P:QUADRANT, :].bitcast(I32), picked[BLOCK_PARTITIONS * i:P:QUADRANT, :].bitcast(I32)
                )

        def entries(held, cols):
            return held[:, cols.start // LIST_ROWS:cols.stop // LIST_ROWS]

        dw_table = keep.tile([P, G], U32, name="dw_table", align_bytes=64)
        xw_table = keep.tile([P, T], U32, name="xw_table", align_bytes=64)
        load_words(nc.scalar, dw_table, d_words, slice(0, DW_FIRST))
        xs_table = load_scales("xs_table", x_scales, T)
        offs_list = load_list("offs_list", offs)
        k1_list = load_list("k1_list", k1)
        ds_table = load_scales("ds_table", d_scales, G)
        load_words(nc.sync, dw_table, d_words, slice(DW_FIRST, G))
        load_words(nc.sync, xw_table, x_words, slice(0, T))
        first_plane = zeroed_bytes("first_plane", H + S)
        cand_plane = zeroed_bytes("cand_plane", C)

        first_picked = keep.tile([P, H + S], U8, name="first_picked", align_bytes=64)
        nc.vector.tensor_copy(out=first_picked[:, H:], in_=xs_table[:].indirect(offs_list[:]))
        nc.vector.tensor_copy(out=first_picked[:, :H], in_=ds_table[:].indirect(k1_list[:]))
        place_scale_rows(first_plane, first_picked, (nc.sync, nc.scalar))
        n1_list = load_list("n1_list", n1)
        n2_list = load_list("n2_list", n2)
        cand_list = load_list("cand_list", cand)
        n3_list = load_list("n3_list", n3)
        gain = keep.tile([P, PACK], F32, name="gain")
        nc.sync.dma_start(gain[:], gs.rearrange("(p t) o -> p (t o)", t=PACK))
        n4_list = load_list("n4_list", n4)
        n5_list = load_list("n5_list", n5)

        dw_picked = keep.tile([P, H], U32, name="dw_picked", tag="ds_table", align_bytes=64)
        nc.vector.tensor_copy(out=dw_picked[:], in_=dw_table[:].indirect(k1_list[:]))
        dw_by_slot = dw_picked[:].rearrange("p (m t) -> p t m", t=PACK)
        ds_by_slot = first_plane[:, :H].rearrange("p (m t) -> p t m", t=PACK)
        dw_first = keep.tile([P, P], U32, name="dw_first", align_bytes=64)
        nc.vector.tensor_copy(out=dw_first[:], in_=dw_by_slot[:, 0, :])
        xq_words = keep.tile([P, S], U32, name="xq_words", align_bytes=64)
        nc.vector.tensor_copy(out=xq_words[:], in_=xw_table[:].indirect(offs_list[:]))
        ds_dealt = keep.tile([P, PACK, P], U8, name="ds_dealt", align_bytes=64)
        dw_rest = keep.tile([P, PACK - 1, P], U32, name="dw_rest", tag="first_picked", align_bytes=64)
        dw_dealt = [dw_first[:]] + [dw_rest[:, t, :] for t in range(PACK - 1)]

        h_rows = []
        for t in range(PACK):
            nc.vector.tensor_copy(out=ds_dealt[:, t, :], in_=ds_by_slot[:, t, :])
            if t > 0:
                nc.vector.tensor_copy(out=dw_dealt[t], in_=dw_by_slot[:, t, :])
            bank = psum.tile([P, S], F32, name=f"h_bank{t}", tag=f"bank{t}")
            nc.tensor.matmul_mx(
                out=bank[:],
                lhsT=dw_dealt[t].bitcast(FP8X4),
                lhsT_scale=ds_dealt[:, t, :],
                rhs=xq_words[:].bitcast(FP8X4),
                rhs_scale=first_plane[:, H:],
                start=True,
                stop=True,
            )
            h = keep.tile([P, S], F32, name=f"h{t}")
            if t == 0:
                nc.scalar.activation(out=h[:], in_=bank[:], func=COPY, scale=SIXTEENTH)
            else:
                nc.vector.tensor_scalar(out=h[:], in0=bank[:], scalar1=SIXTEENTH, scalar2=None, op0=ALU.mult)
            h_rows.append(h)

        mixed = {}
        dt_rows = {}

        def fetch_pairs(t):
            pa = keep.tile([P, W], F32, name=f"pa{t}", align_bytes=64)
            pb = keep.tile([P, W], F32, name=f"pb{t}", align_bytes=64)
            nc.scalar.activation(out=pa[:], in_=h_rows[t][:].indirect(n1_list[:]), func=COPY)
            nc.scalar.activation(out=pb[:], in_=h_rows[t][:].indirect(n2_list[:]), func=COPY)
            for side, op in enumerate((ALU.add, ALU.subtract)):
                mixed[t, side] = keep.tile([P, W], F32, name=f"mix{t}_{side}")
                nc.vector.tensor_tensor(out=mixed[t, side][:], in0=pa[:], in1=pb[:], op=op)

        def send_pair(t, side):
            if side == 0:
                tag = f"dt{t}" if t < 2 else f"mix{t - 2}_1"
                dt_rows[t] = keep.tile([P, S], F32, name=f"dt{t}", tag=tag)
            places = (n1_list, n2_list)[side]
            nc.scalar.activation(out=dt_rows[t][:].indirect(places[:]), in_=mixed[t, side][:], func=COPY)

        def larger_of(t, cols, other, larger):
            nc.scalar.activation(out=other, in_=dt_rows[t][:].indirect(entries(n3_list, cols)), func=COPY)
            nc.vector.tensor_tensor(out=larger, in0=other, in1=dt_rows[t][:, cols], op=ALU.max)

        def weigh(t, larger, z):
            nc.vector.tensor_scalar(out=z, in0=larger, scalar1=gain[:, t:t + 1], scalar2=None, op0=ALU.mult)

        z_plane = keep.tile([P, S], U8, name="z_plane", align_bytes=64)
        z_words = {}

        def quantise(cols, z):
            words = keep.tile([P, cols.stop - cols.start], U32, name=f"z_words{cols.start}", align_bytes=64)
            nc.vector.quantize_mx(
                out=words[:].bitcast(FP8X4), scales=z_plane[:, cols], in_=z.rearrange("p j t -> p (j t)")
            )
            z_words[cols.start] = words

        early = slice(0, EARLY)
        late = slice(EARLY, S)
        late_parts = (slice(EARLY, 2 * EARLY), slice(2 * EARLY, S))
        early_z = keep.tile([P, EARLY, PACK], BF16, name="early_z", align_bytes=64)

        def make_early_z(slots):
            larger = {}
            for t in slots:
                other = keep.tile([P, EARLY], F32, name=f"early_other{t}")
                larger[t] = keep.tile([P, EARLY], F32, name=f"early_larger{t}")
                larger_of(t, early, other[:], larger[t][:])
            for t in slots:
                weigh(t, larger[t][:], early_z[:, :, t])

        fetch_pairs(0)
        fetch_pairs(1)
        cand_picked = keep.tile([P, C], U8, name="cand_picked", tag="pb1", align_bytes=64)
        nc.vector.tensor_copy(out=cand_picked[:], in_=xs_table[:].indirect(cand_list[:]))
        place_scale_rows(cand_plane, cand_picked, (nc.sync,))
        for side in range(2):
            send_pair(0, side)
            send_pair(1, side)
        fetch_pairs(2)
        cand_words = keep.tile([P, C], U32, name="cand_words", tag="pb2", align_bytes=64)
        nc.vector.tensor_copy(out=cand_words[:], in_=xw_table[:].indirect(cand_list[:]))
        fetch_pairs(3)
        make_early_z((0,))
        send_pair(2, 0)
        make_early_z((1,))
        send_pair(3, 0)
        send_pair(2, 1)
        send_pair(3, 1)
        make_early_z((2, 3))
        quantise(early, early_z[:])

        scores = [keep.tile([P, S], F32, name=f"scores{c}") for c in range(BLOCKS)]

        def score(c, parts, bank_tag, on_scalar):
            first, last = parts[0].start, parts[-1].stop
            bank = psum.tile([P, last - first], F32, name=f"s_bank{c}_{first}", tag=bank_tag)
            for cols in parts:
                nc.tensor.matmul_mx(
                    out=bank[:, cols.start - first:cols.stop - first],
                    lhsT=cand_words[:, P * c:P * (c + 1)].bitcast(FP8X4),
                    lhsT_scale=cand_plane[:, P * c:P * (c + 1)],
                    rhs=z_words[cols.start][:].bitcast(FP8X4),
                    rhs_scale=z_plane[:, cols],
                    start=True,
                    stop=True,
                )
            if on_scalar:
                nc.scalar.activation(out=scores[c][:, first:last], in_=bank[:], func=COPY, scale=SIXTEENTH)
            else:
                nc.vector.tensor_scalar(
                    out=scores[c][:, first:last], in0=bank[:], scalar1=SIXTEENTH, scalar2=None, op0=ALU.mult
                )

        sent = [[keep.tile([P, S], F32, name=f"sent{c}_{side}") for side in range(2)] for c in range(BLOCKS)]

        def send_scores(c, cols):
            for side, places in enumerate((n4_list, n5_list)):
                nc.scalar.activation(
                    out=sent[c][side][:].indirect(entries(places, cols)), in_=scores[c][:, cols], func=COPY
                )

        for c in range(BLOCKS):
            score(c, (early,), f"bank{c}", c < SCALAR_EMPTIES)

        late_other = keep.tile([P, PACK, LATE], F32, name="late_other", tag=f"early_other{PACK - 1}")
        late_larger = keep.tile([P, PACK, LATE], F32, name="late_larger", tag="early_z", align_bytes=64)
        late_rows = keep.tile([P, PACK, LATE], BF16, name="late_rows")
        late_z = keep.tile([P, LATE, PACK], BF16, name="late_z", tag=f"z_words{early.start}", align_bytes=64)
        for t in range(PACK):
            larger_of(t, late, late_other[:, t, :], late_larger[:, t, :])
            weigh(t, late_larger[:, t, :], late_rows[:, t, :])
        nc.vector.tensor_copy(
            out=late_z[:].rearrange("p (c i) t -> p c t i", i=4),
            in_=late_rows[:].rearrange("p t (c i) -> p c t i", i=4),
        )
        for cols in late_parts:
            quantise(cols, late_z[:, cols.start - EARLY:cols.stop - EARLY, :])

        for c in range(BLOCKS):
            send_scores(c, early)
        for c in range(BLOCKS):
            score(c, late_parts, "late_bank", False)
        for c in range(BLOCKS):
            send_scores(c, late)
            result = keep.tile([P, S], F32, name=f"result{c}")
            nc.vector.tensor_tensor(out=result[:], in0=sent[c][0][:], in1=sent[c][1][:], op=ALU.max)
            nc.sync.dma_start(out[P * c:P * (c + 1), :], result[:])
